import numpy as np
import ml_dtypes


def mxq(x, axis, fmt="e4m3"):
    dtype, down = {"e4m3": (ml_dtypes.float8_e4m3fn, 7), "e5m2": (ml_dtypes.float8_e5m2, 14)}[fmt]
    v = np.moveaxis(np.asarray(x, np.float32).astype(ml_dtypes.bfloat16).astype(np.float64), axis, -1)
    blocks = v.reshape(v.shape[:-1] + (-1, 32))
    amax = np.abs(blocks).max(-1, keepdims=True)
    byte = np.maximum(np.where(amax > 0, np.frexp(amax)[1] - 1 + 127, 0) - down, 1)
    scale = np.exp2(byte - 127.0)
    codes = (blocks / scale).astype(np.float32).astype(dtype).astype(np.float64)
    return np.moveaxis((codes * scale).reshape(v.shape), -1, axis)


WIDE = False


def mx_kscale(k):
    if not WIDE:
        return np.ones(k)
    levels = np.array([24, -24, 12, -12, 0])
    if k % 512:
        return np.exp2(np.random.permutation(np.resize(levels, k // 32))).repeat(32)
    a = np.empty((k // 512, 16))
    for p in range(k // 512):
        a[p, :8] = np.random.permutation(np.resize(levels, 8))
        for g in range(8):
            far = levels[np.abs(levels - a[p, g]) >= 10]
            a[p, g + 8] = far[np.random.randint(len(far))]
    return np.exp2(a.ravel()).repeat(32)


def f64(x):
    return np.asarray(x).astype(np.float64)


def striped(idx):
    return np.tile(idx.reshape(-1, 16).T, (8, 1)).astype(np.uint16)


def unstriped(offs):
    return offs[:16].T.reshape(-1).astype(np.int64)


E2M1 = np.array([0.0, 0.5, 1.0, 1.5, 2.0, 3.0, 4.0, 6.0, -0.0, -0.5, -1.0, -1.5, -2.0, -3.0, -4.0, -6.0])


def pack_weight(w, fmt):
    k, n = w.shape
    w = f64(np.asarray(w, np.float32).astype(ml_dtypes.bfloat16)).reshape(k // 32, 32, n)
    amax = np.abs(w).max(1)
    if fmt == "e4m3":
        byte = np.frexp(amax)[1] - 1 + 127 - 7
    else:
        mant, ex = np.frexp(amax / 6.0)
        byte = np.where(mant > 0.5, ex, ex - 1) + 127
    byte = np.clip(np.where(amax > 0, byte, 1), 1, 254)
    scaled = (w * np.exp2(127.0 - byte)[:, None, :]).reshape(k, n).astype(np.float32)
    by_word = np.ascontiguousarray(scaled.reshape(k // 512, 128, 4, n).transpose(0, 1, 3, 2))
    if fmt == "e4m3":
        words = by_word.astype(ml_dtypes.float8_e4m3fn).view(np.uint8)
    else:
        c = by_word.astype(ml_dtypes.float4_e2m1fn).view(np.uint8) & 0xF
        words = (c[..., 0::2] | (c[..., 1::2] << 4)).reshape(k // 512, 128, 2 * n)
    return np.ascontiguousarray(words), np.ascontiguousarray(byte.astype(np.uint8).reshape(k // 512, 16, n))


def unpack_weight(words, scales, fmt):
    g, _, n = scales.shape
    words = np.ascontiguousarray(words).reshape(g, 128, n, -1)
    if fmt == "e4m3":
        vals = words.view(ml_dtypes.float8_e4m3fn).astype(np.float64)
    else:
        nib = np.empty((g, 128, n, 4), np.uint8)
        nib[..., 0::2] = words & 0xF
        nib[..., 1::2] = words >> 4
        vals = E2M1[nib]
    vals = vals * np.repeat(np.exp2(scales.astype(np.float64) - 127.0), 8, axis=1)[..., None]
    return vals.transpose(0, 1, 3, 2).reshape(g * 512, n)


K, M, N, T, J = 1024, 512, 512, 2048, 1024


def setup_inputs():
    n = np.random.standard_normal
    s = mx_kscale(K)[:, None]
    s2 = mx_kscale(M)[:, None]
    h = np.tanh(n((N, T)))
    p_tab = pack_weight(h * s2, "e4m3")
    return {
        "x": (n((K, J)) * s).astype(np.float32),
        "tab_words": p_tab[0],
        "tab_scales": p_tab[1],
        "wn": (n((K, N)) / np.sqrt(K) / s).astype(np.float32),
        "un": (n((M, N)) / np.sqrt(M) / s2).astype(np.float32),
        "bn": (0.3 * n(N)).astype(np.float32),
        "hT": (h).astype(np.float32),
        "wgo": np.tile(np.random.uniform(0.5, 2.0, J), (128, 1)).astype(np.float32),
        "offs": striped(np.random.permutation(T)[:J]),
    }


def reference(x, tab_words, tab_scales, wn, un, bn, hT, wgo, offs):
    idx = unstriped(offs)
    x_ = mxq(f64(x), 0, "e4m3")
    tab_ = unpack_weight(tab_words, tab_scales, "e4m3")[:, idx]
    wn_ = mxq(f64(wn), 0, "e4m3")
    un_ = mxq(f64(un), 0, "e4m3")
    sn = wn_.T @ x_ + un_.T @ tab_
    out = np.zeros((N, T))
    out[:, idx] = f64(wgo)[0] * (np.tanh(sn + f64(bn)[:, None]) + f64(hT)[:, idx])
    return out

@@ -1,0 +1,198 @@
+from contextlib import ExitStack
+
+import concourse.mybir as mybir
+
+K, M, N, T, J = 1024, 512, 512, 2048, 1024
+FLOPS = 2 * (K + M) * N * J
+
+F32 = mybir.dt.float32
+BF16 = mybir.dt.bfloat16
+I32 = mybir.dt.int32
+U32 = mybir.dt.uint32
+U16 = mybir.dt.uint16
+U8 = mybir.dt.uint8
+FP8X4 = mybir.dt.float8_e4m3fn_x4
+ADD = mybir.AluOpType.add
+MULT = mybir.AluOpType.mult
+TANH = mybir.ActivationFunctionType.Tanh
+
+P = 128
+PACK = 4
+K_PASS = P * PACK
+N_TILES = N // P
+Q = 256
+
+
+def tile_list_tgn_rnn_kernel(tc, x, tab_words, tab_scales, wn, un, bn, hT, wgo, offs, out):
+    nc = tc.nc
+    with ExitStack() as ctx:
+        keep = ctx.enter_context(tc.tile_pool(name="keep", bufs=1))
+        psum = ctx.enter_context(tc.psum_pool(name="psum", bufs=6))
+
+        def tile(name, shape, dtype, tag=None):
+            return keep.tile(shape, dtype, name=name, tag=tag or name, align_bytes=64)
+
+        offsets = keep.tile([P, J // 16], U16, name="offsets")
+        nc.sync.dma_start(offsets[:], offs)
+
+        plane = tile("plane", [P, T], U8)
+        nc.vector.memset(plane[:].bitcast(I32), 0)
+        warm_in = tile("warm_in", [P, 1], F32)
+        warm_out = tile("warm_out", [P, 1], F32)
+        nc.gpsimd.memset(warm_in[:], 0.0)
+        nc.scalar.activation(out=warm_out[:], in_=warm_in[:], func=TANH)
+
+        table = tile("table", [P, T], I32)
+        nc.sync.dma_start(out=table[:], in_=tab_words[0].rearrange("p t i -> p (t i)").bitcast(I32))
+        for q in range(4):
+            nc.sync.dma_start(
+                out=plane[32 * q : 32 * q + 4, :].bitcast(I32),
+                in_=tab_scales[0, 4 * q : 4 * q + 4, :].bitcast(I32),
+            )
+        bias = tile("bias", [P, N_TILES], F32)
+        with nc.allow_non_contiguous_dma(reason="one bias value for each partition and tile"):
+            nc.gpsimd.dma_start(out=bias[:], in_=bn.rearrange("(c p) -> p c", p=P))
+
+        pages = [tile("page%d" % c, [P, T], F32) for c in range(N_TILES)]
+        for page in pages:
+            nc.vector.memset(page[:], 0.0)
+
+        def load_rows(name, rows):
+            raw = tile(name, [P, PACK, rows.shape[1]], F32)
+            nc.sync.dma_start(out=raw[:], in_=rows.rearrange("(p j) w -> p j w", j=PACK))
+            return raw
+
+        def load_w(c):
+            cols = slice(c * P, (c + 1) * P)
+            srcs = [un[:, cols], wn[0:K_PASS, cols], wn[K_PASS:K, cols]]
+            return [load_rows("w%d_%d" % (c, a), s) for a, s in enumerate(srcs)]
+
+        def load_x(a, j0, j1):
+            return load_rows("x%d_%d" % (a, j0), x[a * K_PASS : (a + 1) * K_PASS, j0:j1])
+
+        def load_h(c):
+            h = tile("h%d" % c, [P, T], F32)
+            nc.sync.dma_start(out=h[:], in_=hT[c * P : (c + 1) * P, :])
+            return h
+
+        gain = tile("gain", [P, J], F32)
+        w_raw, h_in, x_raw = {}, {}, {}
+        w_raw[0] = load_w(0)
+        x_raw[0, 0] = load_x(0, 0, 2 * Q)
+        x_raw[1, 0] = load_x(1, 0, Q)
+        x_raw[1, Q] = load_x(1, Q, 2 * Q)
+        h_in[0] = load_h(0)
+        nc.sync.dma_start(out=gain[:, 0:Q], in_=wgo[:, 0:Q])
+        w_raw[1] = load_w(1)
+        nc.sync.dma_start(out=gain[:, Q:J], in_=wgo[:, Q:J])
+        h_in[1] = load_h(1)
+        for j0 in (2 * Q, 3 * Q):
+            for a in range(2):
+                x_raw[a, j0] = load_x(a, j0, j0 + Q)
+        w_raw[2] = load_w(2)
+        w_raw[3] = load_w(3)
+        h_in[2] = load_h(2)
+        h_in[3] = load_h(3)
+
+        def weave(name, raw, on_vector, tag=None):
+            width = raw.shape[2]
+            woven = tile(name, [P, width, PACK], BF16, tag)
+            dst = woven[:].rearrange("p (c i) t -> p c t i", i=4)
+            src = raw[:].rearrange("p t (c i) -> p c t i", i=4)
+            if on_vector:
+                nc.vector.tensor_copy(out=dst, in_=src)
+            else:
+                nc.scalar.copy(out=dst, in_=src)
+            return woven
+
+        def quantise(woven, codes, scales):
+            nc.vector.quantize_mx(
+                out=codes.bitcast(FP8X4), scales=scales, in_=woven[:].rearrange("p w t -> p (w t)")
+            )
+
+        x_codes = [tile("x_codes%d" % a, [P, J], U32) for a in range(2)]
+        x_scales = [tile("x_scales%d" % a, [P, J], U8) for a in range(2)]
+        w_codes, w_scales = {}, {}
+
+        def prepare_w(c, tag=None):
+            for a in range(3):
+                woven = weave("ww%d_%d" % (c, a), w_raw[c][a], False, tag if a == 2 else None)
+                w_codes[c, a] = tile("w_codes%d_%d" % (c, a), [P, P], U32)
+                w_scales[c, a] = tile("w_scales%d_%d" % (c, a), [P, P], U8)
+                quantise(woven, w_codes[c, a][:], w_scales[c, a][:])
+
+        def prepare_x(a, j0, on_vector, tag=None):
+            raw = x_raw[a, j0]
+            cols = slice(j0, j0 + raw.shape[2])
+            woven = weave("xw%d_%d" % (a, j0), raw, on_vector, tag)
+            quantise(woven, x_codes[a][:, cols], x_scales[a][:, cols])
+
+        def picks(j0, j1):
+            return offsets[:, j0 // 16 : j1 // 16]
+
+        v_codes = tile("v_codes", [P, J], U32)
+        v_scales = tile("v_scales", [P, J], U8)
+        nc.vector.tensor_copy(out=v_codes[:], in_=table[:].bitcast(U32).indirect(offsets[:]))
+        prepare_w(0)
+        nc.vector.tensor_copy(out=v_scales[:], in_=plane[:].indirect(offsets[:]))
+        prepare_x(0, 0, False)
+        prepare_x(1, 0, True)
+        prepare_x(1, Q, True)
+
+        acts = [tile("act%d" % c, [P, J], F32) for c in range(N_TILES)]
+
+        def product(c, j0, j1):
+            cols = slice(j0, j1)
+            acc = psum.tile([P, j1 - j0], F32, name="acc")
+            moving = [(v_codes, v_scales), (x_codes[0], x_scales[0]), (x_codes[1], x_scales[1])]
+            for a, (codes, scales) in enumerate(moving):
+                nc.tensor.matmul_mx(
+                    out=acc[:],
+                    lhsT=w_codes[c, a][:].bitcast(FP8X4),
+                    lhsT_scale=w_scales[c, a][:],
+                    rhs=codes[:, cols].bitcast(FP8X4),
+                    rhs_scale=scales[:, cols],
+                    start=(a == 0),
+                    stop=(a == 2),
+                )
+            nc.scalar.activation(out=acts[c][:, cols], in_=acc[:], func=TANH, bias=bias[:, c : c + 1])
+
+        def place(c, j0, j1, tag=None):
+            summed = tile("sum%d_%d" % (c, j0), [P, j1 - j0], F32, tag)
+            nc.vector.tensor_tensor(summed[:], h_in[c][:].indirect(picks(j0, j1)), acts[c][:, j0:j1], ADD)
+            nc.vector.tensor_tensor(pages[c][:].indirect(picks(j0, j1)), summed[:], gain[:, j0:j1], MULT)
+
+        def store(c):
+            nc.sync.dma_start(out=out[c * P : (c + 1) * P, :], in_=pages[c][:])
+
+        product(0, 0, 2 * Q)
+        place(0, 0, Q)
+        prepare_w(1, "hold_w1")
+        product(1, 0, 2 * Q)
+        place(0, Q, 2 * Q, "hold_w1")
+        place(1, 0, Q)
+        prepare_x(0, 2 * Q, False)
+        prepare_x(1, 2 * Q, False, "hold_xc")
+        product(0, 2 * Q, 3 * Q)
+        product(1, 2 * Q, 3 * Q)
+        place(1, Q, 2 * Q, "hold_xc")
+        place(1, 2 * Q, 3 * Q)
+        prepare_x(0, 3 * Q, False)
+        prepare_x(1, 3 * Q, False, "hold_xd")
+        product(0, 3 * Q, J)
+        product(1, 3 * Q, J)
+        place(0, 2 * Q, 3 * Q, "hold_xd")
+        prepare_w(2, "hold_w2")
+        product(2, 0, 2 * Q)
+        product(2, 2 * Q, J)
+        place(0, 3 * Q, J, "hold_w2")
+        store(0)
+        prepare_w(3, "hold_w3")
+        product(3, 0, 2 * Q)
+        product(3, 2 * Q, J)
+        place(1, 3 * Q, J, "hold_w3")
+        store(1)
+        place(2, 0, J)
+        store(2)
+        place(3, 0, J)
+        store(3)

@@ -39,33 +39,35 @@ def tile_list_tgn_rnn_kernel(tc, x, tab_words, tab_scales, wn, un, bn, hT, wgo, 
         nc.vector.memset(plane[:].bitcast(I32), 0)
         warm_in = tile("warm_in", [P, 1], F32)
         warm_out = tile("warm_out", [P, 1], F32)
-        nc.gpsimd.memset(warm_in[:], 0.0)
+        nc.vector.memset(warm_in[:], 0.0)
         nc.scalar.activation(out=warm_out[:], in_=warm_in[:], func=TANH)
 
-        table = tile("table", [P, T], I32)
-        nc.sync.dma_start(out=table[:], in_=tab_words[0].rearrange("p t i -> p (t i)").bitcast(I32))
+        landed = [tile("landed%d" % q, [P, T // 4], I32) for q in range(4)]
         for q in range(4):
             nc.sync.dma_start(
-                out=plane[32 * q : 32 * q + 4, :].bitcast(I32),
+                out=landed[q][32 * q : 32 * q + 4, :],
                 in_=tab_scales[0, 4 * q : 4 * q + 4, :].bitcast(I32),
             )
+        table = tile("table", [P, T], I32)
+        nc.sync.dma_start(out=table[:], in_=tab_words[0].rearrange("p t i -> p (t i)").bitcast(I32))
         bias = tile("bias", [P, N_TILES], F32)
         with nc.allow_non_contiguous_dma(reason="one bias value for each partition and tile"):
             nc.gpsimd.dma_start(out=bias[:], in_=bn.rearrange("(c p) -> p c", p=P))
 
-        pages = [tile("page%d" % c, [P, T], F32) for c in range(N_TILES)]
-        for page in pages:
-            nc.vector.memset(page[:], 0.0)
 
         def load_rows(name, rows):
             raw = tile(name, [P, PACK, rows.shape[1]], F32)
             nc.sync.dma_start(out=raw[:], in_=rows.rearrange("(p j) w -> p j w", j=PACK))
-            return raw
+            return raw[:]
 
         def load_w(c):
             cols = slice(c * P, (c + 1) * P)
             srcs = [un[:, cols], wn[0:K_PASS, cols], wn[K_PASS:K, cols]]
-            return [load_rows("w%d_%d" % (c, a), s) for a, s in enumerate(srcs)]
+            raw = tile("w%d" % c, [P, 3 * PACK, P], F32)
+            parts = [raw[:, a * PACK : (a + 1) * PACK, :] for a in range(3)]
+            for part, rows in zip(parts, srcs):
+                nc.sync.dma_start(out=part, in_=rows.rearrange("(p j) w -> p j w", j=PACK))
+            return parts
 
         def load_x(a, j0, j1):
             return load_rows("x%d_%d" % (a, j0), x[a * K_PASS : (a + 1) * K_PASS, j0:j1])
@@ -77,122 +79,126 @@ def tile_list_tgn_rnn_kernel(tc, x, tab_words, tab_scales, wn, un, bn, hT, wgo, 
 
         gain = tile("gain", [P, J], F32)
         w_raw, h_in, x_raw = {}, {}, {}
+
+        def load_x_quarter(b):
+            x_raw[b] = [load_x(a, b * Q, (b + 1) * Q) for a in range(2)]
+
         w_raw[0] = load_w(0)
-        x_raw[0, 0] = load_x(0, 0, 2 * Q)
-        x_raw[1, 0] = load_x(1, 0, Q)
-        x_raw[1, Q] = load_x(1, Q, 2 * Q)
+        load_x_quarter(0)
+        load_x_quarter(1)
         h_in[0] = load_h(0)
         nc.sync.dma_start(out=gain[:, 0:Q], in_=wgo[:, 0:Q])
         w_raw[1] = load_w(1)
         nc.sync.dma_start(out=gain[:, Q:J], in_=wgo[:, Q:J])
         h_in[1] = load_h(1)
-        for j0 in (2 * Q, 3 * Q):
-            for a in range(2):
-                x_raw[a, j0] = load_x(a, j0, j0 + Q)
+        load_x_quarter(2)
+        load_x_quarter(3)
         w_raw[2] = load_w(2)
         w_raw[3] = load_w(3)
         h_in[2] = load_h(2)
         h_in[3] = load_h(3)
 
-        def weave(name, raw, on_vector, tag=None):
-            width = raw.shape[2]
-            woven = tile(name, [P, width, PACK], BF16, tag)
-            dst = woven[:].rearrange("p (c i) t -> p c t i", i=4)
-            src = raw[:].rearrange("p t (c i) -> p c t i", i=4)
-            if on_vector:
-                nc.vector.tensor_copy(out=dst, in_=src)
-            else:
-                nc.scalar.copy(out=dst, in_=src)
-            return woven
-
-        def quantise(woven, codes, scales):
-            nc.vector.quantize_mx(
-                out=codes.bitcast(FP8X4), scales=scales, in_=woven[:].rearrange("p w t -> p (w t)")
-            )
+        def weave_and_quantise(name, raws, codes, scales, tag):
+            width = raws[0].shape[2] * PACK
+            woven = tile(name, [P, len(raws) * width], BF16, tag)
+            for a, raw in enumerate(raws):
+                part = woven[:, a * width : (a + 1) * width]
+                nc.scalar.copy(
+                    out=part.rearrange("p (c i t) -> p c t i", i=4, t=PACK),
+                    in_=raw.rearrange("p t (c i) -> p c t i", i=4),
+                )
+                nc.vector.quantize_mx(out=codes[a].bitcast(FP8X4), scales=scales[a], in_=part)
 
         x_codes = [tile("x_codes%d" % a, [P, J], U32) for a in range(2)]
         x_scales = [tile("x_scales%d" % a, [P, J], U8) for a in range(2)]
         w_codes, w_scales = {}, {}
 
         def prepare_w(c, tag=None):
-            for a in range(3):
-                woven = weave("ww%d_%d" % (c, a), w_raw[c][a], False, tag if a == 2 else None)
-                w_codes[c, a] = tile("w_codes%d_%d" % (c, a), [P, P], U32)
-                w_scales[c, a] = tile("w_scales%d_%d" % (c, a), [P, P], U8)
-                quantise(woven, w_codes[c, a][:], w_scales[c, a][:])
+            w_codes[c] = [tile("w_codes%d_%d" % (c, a), [P, P], U32) for a in range(3)]
+            w_scales[c] = [tile("w_scales%d_%d" % (c, a), [P, P], U8) for a in range(3)]
+            weave_and_quantise("ww%d" % c, w_raw[c], [t[:] for t in w_codes[c]], [t[:] for t in w_scales[c]], tag)
 
-        def prepare_x(a, j0, on_vector, tag=None):
-            raw = x_raw[a, j0]
-            cols = slice(j0, j0 + raw.shape[2])
-            woven = weave("xw%d_%d" % (a, j0), raw, on_vector, tag)
-            quantise(woven, x_codes[a][:, cols], x_scales[a][:, cols])
+        def prepare_x(b, tag=None):
+            cols = slice(b * Q, (b + 1) * Q)
+            weave_and_quantise(
+                "xw%d" % b, x_raw[b], [t[:, cols] for t in x_codes], [t[:, cols] for t in x_scales], tag
+            )
 
         def picks(j0, j1):
             return offsets[:, j0 // 16 : j1 // 16]
 
         v_codes = tile("v_codes", [P, J], U32)
         v_scales = tile("v_scales", [P, J], U8)
+        for q in range(4):
+            rows = slice(32 * q, 32 * q + 4)
+            nc.vector.tensor_copy(out=plane[rows, :].bitcast(I32), in_=landed[q][rows, :])
+        nc.vector.tensor_copy(out=v_scales[:], in_=plane[:].indirect(offsets[:]))
         nc.vector.tensor_copy(out=v_codes[:], in_=table[:].bitcast(U32).indirect(offsets[:]))
         prepare_w(0)
-        nc.vector.tensor_copy(out=v_scales[:], in_=plane[:].indirect(offsets[:]))
-        prepare_x(0, 0, False)
-        prepare_x(1, 0, True)
-        prepare_x(1, Q, True)
+        prepare_x(0, "w0")
+        prepare_x(1, "x1_0")
+        pages = [tile("page0", [P, T], F32), tile("page1", [P, T], F32)]
+        nc.vector.memset(pages[0][:], 0.0)
+        nc.gpsimd.memset(pages[1][:], 0.0)
+        pages = pages + pages
 
-        acts = [tile("act%d" % c, [P, J], F32) for c in range(N_TILES)]
+        acts = {}
 
-        def product(c, j0, j1):
-            cols = slice(j0, j1)
-            acc = psum.tile([P, j1 - j0], F32, name="acc")
-            moving = [(v_codes, v_scales), (x_codes[0], x_scales[0]), (x_codes[1], x_scales[1])]
-            for a, (codes, scales) in enumerate(moving):
-                nc.tensor.matmul_mx(
-                    out=acc[:],
-                    lhsT=w_codes[c, a][:].bitcast(FP8X4),
-                    lhsT_scale=w_scales[c, a][:],
-                    rhs=codes[:, cols].bitcast(FP8X4),
-                    rhs_scale=scales[:, cols],
-                    start=(a == 0),
-                    stop=(a == 2),
+        def product(c, j0, j1, tag=None):
+            acts[c, j0] = tile("act%d_%d" % (c, j0), [P, j1 - j0], F32, tag)
+            step = min(j1 - j0, 2 * Q)
+            for n0 in range(j0, j1, step):
+                cols = slice(n0, n0 + step)
+                acc = psum.tile([P, step], F32, name="acc")
+                moving = [(v_codes, v_scales), (x_codes[0], x_scales[0]), (x_codes[1], x_scales[1])]
+                for a, (codes, scales) in enumerate(moving):
+                    nc.tensor.matmul_mx(
+                        out=acc[:],
+                        lhsT=w_codes[c][a][:].bitcast(FP8X4),
+                        lhsT_scale=w_scales[c][a][:],
+                        rhs=codes[:, cols].bitcast(FP8X4),
+                        rhs_scale=scales[:, cols],
+                        start=(a == 0),
+                        stop=(a == 2),
+                    )
+                nc.scalar.activation(
+                    out=acts[c, j0][:, n0 - j0 : n0 - j0 + step], in_=acc[:], func=TANH, bias=bias[:, c : c + 1]
                 )
-            nc.scalar.activation(out=acts[c][:, cols], in_=acc[:], func=TANH, bias=bias[:, c : c + 1])
 
         def place(c, j0, j1, tag=None):
             summed = tile("sum%d_%d" % (c, j0), [P, j1 - j0], F32, tag)
-            nc.vector.tensor_tensor(summed[:], h_in[c][:].indirect(picks(j0, j1)), acts[c][:, j0:j1], ADD)
+            nc.vector.tensor_tensor(summed[:], h_in[c][:].indirect(picks(j0, j1)), acts[c, j0][:], ADD)
             nc.vector.tensor_tensor(pages[c][:].indirect(picks(j0, j1)), summed[:], gain[:, j0:j1], MULT)
 
         def store(c):
             nc.sync.dma_start(out=out[c * P : (c + 1) * P, :], in_=pages[c][:])
 
-        product(0, 0, 2 * Q)
+        product(0, 0, Q, "hold_w1")
+        product(0, Q, 2 * Q)
         place(0, 0, Q)
         prepare_w(1, "hold_w1")
-        product(1, 0, 2 * Q)
+        product(1, 0, Q, "hold_xc")
+        product(1, Q, 2 * Q)
         place(0, Q, 2 * Q, "hold_w1")
-        place(1, 0, Q)
-        prepare_x(0, 2 * Q, False)
-        prepare_x(1, 2 * Q, False, "hold_xc")
-        product(0, 2 * Q, 3 * Q)
-        product(1, 2 * Q, 3 * Q)
+        place(1, 0, Q, "hold_xd")
+        prepare_x(2, "hold_xc")
+        product(0, 2 * Q, 3 * Q, "hold_w2")
         place(1, Q, 2 * Q, "hold_xc")
-        place(1, 2 * Q, 3 * Q)
-        prepare_x(0, 3 * Q, False)
-        prepare_x(1, 3 * Q, False, "hold_xd")
-        product(0, 3 * Q, J)
-        product(1, 3 * Q, J)
+        prepare_x(3, "hold_xd")
+        product(0, 3 * Q, J, "hold_w3")
+        product(1, 2 * Q, J)
         place(0, 2 * Q, 3 * Q, "hold_xd")
+        place(0, 3 * Q, J)
+        store(0)
         prepare_w(2, "hold_w2")
         product(2, 0, 2 * Q)
         product(2, 2 * Q, J)
-        place(0, 3 * Q, J, "hold_w2")
-        store(0)
-        prepare_w(3, "hold_w3")
-        product(3, 0, 2 * Q)
-        product(3, 2 * Q, J)
-        place(1, 3 * Q, J, "hold_w3")
+        place(1, 2 * Q, J, "hold_w2")
         store(1)
-        place(2, 0, J)
+        place(2, 0, 2 * Q)
+        prepare_w(3, "hold_w3")
+        product(3, 0, J)
+        place(2, 2 * Q, J, "hold_w3")
         store(2)
         place(3, 0, J)
         store(3)

@@ -42,17 +42,14 @@ def tile_list_tgn_rnn_kernel(tc, x, tab_words, tab_scales, wn, un, bn, hT, wgo, 
         nc.vector.memset(warm_in[:], 0.0)
         nc.scalar.activation(out=warm_out[:], in_=warm_in[:], func=TANH)
 
-        landed = [tile("landed%d" % q, [P, T // 4], I32) for q in range(4)]
-        for q in range(4):
-            nc.sync.dma_start(
-                out=landed[q][32 * q : 32 * q + 4, :],
-                in_=tab_scales[0, 4 * q : 4 * q + 4, :].bitcast(I32),
-            )
+        landed = tile("landed", [P, T // 4], I32)
+        for r in range(4):
+            nc.sync.dma_start(out=landed[r:P:32, :], in_=tab_scales[0, r:16:4, :].bitcast(I32))
         table = tile("table", [P, T], I32)
         nc.sync.dma_start(out=table[:], in_=tab_words[0].rearrange("p t i -> p (t i)").bitcast(I32))
         bias = tile("bias", [P, N_TILES], F32)
         with nc.allow_non_contiguous_dma(reason="one bias value for each partition and tile"):
-            nc.gpsimd.dma_start(out=bias[:], in_=bn.rearrange("(c p) -> p c", p=P))
+            nc.sync.dma_start(out=bias[:], in_=bn.rearrange("(c p) -> p c", p=P))
 
 
         def load_rows(name, rows):
@@ -89,40 +86,45 @@ def tile_list_tgn_rnn_kernel(tc, x, tab_words, tab_scales, wn, un, bn, hT, wgo, 
         h_in[0] = load_h(0)
         nc.sync.dma_start(out=gain[:, 0:Q], in_=wgo[:, 0:Q])
         w_raw[1] = load_w(1)
-        nc.sync.dma_start(out=gain[:, Q:J], in_=wgo[:, Q:J])
+        nc.sync.dma_start(out=gain[:, Q : 2 * Q], in_=wgo[:, Q : 2 * Q])
         h_in[1] = load_h(1)
         load_x_quarter(2)
+        nc.sync.dma_start(out=gain[:, 2 * Q : J], in_=wgo[:, 2 * Q : J])
         load_x_quarter(3)
         w_raw[2] = load_w(2)
         w_raw[3] = load_w(3)
         h_in[2] = load_h(2)
         h_in[3] = load_h(3)
 
-        def weave_and_quantise(name, raws, codes, scales, tag):
+        def weave(name, raws, codes, scales, tag):
             width = raws[0].shape[2] * PACK
             woven = tile(name, [P, len(raws) * width], BF16, tag)
+            steps = []
             for a, raw in enumerate(raws):
                 part = woven[:, a * width : (a + 1) * width]
                 nc.scalar.copy(
                     out=part.rearrange("p (c i t) -> p c t i", i=4, t=PACK),
                     in_=raw.rearrange("p t (c i) -> p c t i", i=4),
                 )
-                nc.vector.quantize_mx(out=codes[a].bitcast(FP8X4), scales=scales[a], in_=part)
+                steps.append((codes[a], scales[a], part))
+            return steps
+
+        def quantise(steps):
+            for codes, scales, part in steps:
+                nc.vector.quantize_mx(out=codes.bitcast(FP8X4), scales=scales, in_=part)
 
         x_codes = [tile("x_codes%d" % a, [P, J], U32) for a in range(2)]
         x_scales = [tile("x_scales%d" % a, [P, J], U8) for a in range(2)]
         w_codes, w_scales = {}, {}
 
-        def prepare_w(c, tag=None):
+        def weave_w(c, tag=None):
             w_codes[c] = [tile("w_codes%d_%d" % (c, a), [P, P], U32) for a in range(3)]
             w_scales[c] = [tile("w_scales%d_%d" % (c, a), [P, P], U8) for a in range(3)]
-            weave_and_quantise("ww%d" % c, w_raw[c], [t[:] for t in w_codes[c]], [t[:] for t in w_scales[c]], tag)
+            return weave("ww%d" % c, w_raw[c], [t[:] for t in w_codes[c]], [t[:] for t in w_scales[c]], tag)
 
-        def prepare_x(b, tag=None):
+        def weave_x(b, tag=None):
             cols = slice(b * Q, (b + 1) * Q)
-            weave_and_quantise(
-                "xw%d" % b, x_raw[b], [t[:, cols] for t in x_codes], [t[:, cols] for t in x_scales], tag
-            )
+            return weave("xw%d" % b, x_raw[b], [t[:, cols] for t in x_codes], [t[:, cols] for t in x_scales], tag)
 
         def picks(j0, j1):
             return offsets[:, j0 // 16 : j1 // 16]
@@ -131,15 +133,15 @@ def tile_list_tgn_rnn_kernel(tc, x, tab_words, tab_scales, wn, un, bn, hT, wgo, 
         v_scales = tile("v_scales", [P, J], U8)
         for q in range(4):
             rows = slice(32 * q, 32 * q + 4)
-            nc.vector.tensor_copy(out=plane[rows, :].bitcast(I32), in_=landed[q][rows, :])
+            nc.vector.tensor_copy(out=plane[rows, :].bitcast(I32), in_=landed[rows, :])
         nc.vector.tensor_copy(out=v_scales[:], in_=plane[:].indirect(offsets[:]))
         nc.vector.tensor_copy(out=v_codes[:], in_=table[:].bitcast(U32).indirect(offsets[:]))
-        prepare_w(0)
-        prepare_x(0, "w0")
-        prepare_x(1, "x1_0")
+        quantise(weave_w(0))
+        quantise(weave_x(0, "w0"))
+        quantise(weave_x(1, "x1_0"))
         pages = [tile("page0", [P, T], F32), tile("page1", [P, T], F32)]
         nc.vector.memset(pages[0][:], 0.0)
-        nc.gpsimd.memset(pages[1][:], 0.0)
+        nc.vector.memset(pages[1][:], 0.0)
         pages = pages + pages
 
         acts = {}
@@ -165,40 +167,56 @@ def tile_list_tgn_rnn_kernel(tc, x, tab_words, tab_scales, wn, un, bn, hT, wgo, 
                     out=acts[c, j0][:, n0 - j0 : n0 - j0 + step], in_=acc[:], func=TANH, bias=bias[:, c : c + 1]
                 )
 
+        sums = {}
+
+        def add_state(c, j0, j1, tag=None):
+            sums[c, j0] = tile("sum%d_%d" % (c, j0), [P, j1 - j0], F32, tag)
+            nc.vector.tensor_tensor(sums[c, j0][:], h_in[c][:].indirect(picks(j0, j1)), acts[c, j0][:], ADD)
+
+        def scatter(c, j0, j1):
+            nc.vector.tensor_tensor(pages[c][:].indirect(picks(j0, j1)), sums[c, j0][:], gain[:, j0:j1], MULT)
+
         def place(c, j0, j1, tag=None):
-            summed = tile("sum%d_%d" % (c, j0), [P, j1 - j0], F32, tag)
-            nc.vector.tensor_tensor(summed[:], h_in[c][:].indirect(picks(j0, j1)), acts[c, j0][:], ADD)
-            nc.vector.tensor_tensor(pages[c][:].indirect(picks(j0, j1)), summed[:], gain[:, j0:j1], MULT)
+            add_state(c, j0, j1, tag)
+            scatter(c, j0, j1)
 
         def store(c):
             nc.sync.dma_start(out=out[c * P : (c + 1) * P, :], in_=pages[c][:])
 
+        def place_round(steps, raw_tag, c, j0, j1):
+            quantise(steps[:-1])
+            add_state(c, j0, j1, raw_tag)
+            quantise(steps[-1:])
+
         product(0, 0, Q, "hold_w1")
         product(0, Q, 2 * Q)
         place(0, 0, Q)
-        prepare_w(1, "hold_w1")
+        place_round(weave_w(1, "hold_w1"), "w1", 0, Q, 2 * Q)
         product(1, 0, Q, "hold_xc")
-        product(1, Q, 2 * Q)
-        place(0, Q, 2 * Q, "hold_w1")
+        product(1, Q, 2 * Q, "hold_w2")
+        scatter(0, Q, 2 * Q)
         place(1, 0, Q, "hold_xd")
-        prepare_x(2, "hold_xc")
-        product(0, 2 * Q, 3 * Q, "hold_w2")
-        place(1, Q, 2 * Q, "hold_xc")
-        prepare_x(3, "hold_xd")
-        product(0, 3 * Q, J, "hold_w3")
+        place_round(weave_x(2, "hold_xc"), "x1_512", 1, Q, 2 * Q)
+        product(0, 2 * Q, 3 * Q, "hold_w3")
+        scatter(1, Q, 2 * Q)
+        place_round(weave_x(3, "hold_xd"), "x1_768", 0, 2 * Q, 3 * Q)
+        product(0, 3 * Q, J)
         product(1, 2 * Q, J)
-        place(0, 2 * Q, 3 * Q, "hold_xd")
-        place(0, 3 * Q, J)
+        scatter(0, 2 * Q, 3 * Q)
+        place_round(weave_w(2, "hold_w2"), "w2", 0, 3 * Q, J)
+        product(2, 0, J)
+        scatter(0, 3 * Q, J)
         store(0)
-        prepare_w(2, "hold_w2")
-        product(2, 0, 2 * Q)
-        product(2, 2 * Q, J)
-        place(1, 2 * Q, J, "hold_w2")
-        store(1)
-        place(2, 0, 2 * Q)
-        prepare_w(3, "hold_w3")
+        quantise(weave_w(3, "hold_w3"))
         product(3, 0, J)
-        place(2, 2 * Q, J, "hold_w3")
+        add_state(1, 2 * Q, J, "w3")
+        add_state(2, 0, J)
+        scatter(1, 2 * Q, J)
+        store(1)
+        add_state(3, 0, J)
+        scatter(2, 0, J)
         store(2)
-        place(3, 0, J)
-        store(3)
+        scatter(3, 0, J)
+        rows = slice(3 * P, N)
+        nc.sync.dma_start(out=out[rows, 0 : T // 2], in_=pages[3][:, 0 : T // 2])
+        nc.scalar.dma_start(out=out[rows, T // 2 : T], in_=pages[3][:, T // 2 : T])

from contextlib import ExitStack

import concourse.mybir as mybir

K, M, N, T, J = 1024, 512, 512, 2048, 1024
FLOPS = 2 * (K + M) * N * J

F32 = mybir.dt.float32
BF16 = mybir.dt.bfloat16
I32 = mybir.dt.int32
U32 = mybir.dt.uint32
U16 = mybir.dt.uint16
U8 = mybir.dt.uint8
FP8X4 = mybir.dt.float8_e4m3fn_x4
ADD = mybir.AluOpType.add
MULT = mybir.AluOpType.mult
TANH = mybir.ActivationFunctionType.Tanh

P = 128
PACK = 4
K_PASS = P * PACK
N_TILES = N // P
Q = 256


def tile_list_tgn_rnn_kernel(tc, x, tab_words, tab_scales, wn, un, bn, hT, wgo, offs, out):
    nc = tc.nc
    with ExitStack() as ctx:
        keep = ctx.enter_context(tc.tile_pool(name="keep", bufs=1))
        psum = ctx.enter_context(tc.psum_pool(name="psum", bufs=6))

        def tile(name, shape, dtype, tag=None):
            return keep.tile(shape, dtype, name=name, tag=tag or name, align_bytes=64)

        offsets = keep.tile([P, J // 16], U16, name="offsets")
        nc.sync.dma_start(offsets[:], offs)

        plane = tile("plane", [P, T], U8)
        nc.vector.memset(plane[:].bitcast(I32), 0)
        warm_in = tile("warm_in", [P, 1], F32)
        warm_out = tile("warm_out", [P, 1], F32)
        nc.vector.memset(warm_in[:], 0.0)
        nc.scalar.activation(out=warm_out[:], in_=warm_in[:], func=TANH)

        landed = tile("landed", [P, T // 4], I32)
        for r in range(4):
            nc.sync.dma_start(out=landed[r:P:32, :], in_=tab_scales[0, r:16:4, :].bitcast(I32))
        table = tile("table", [P, T], I32)
        nc.sync.dma_start(out=table[:], in_=tab_words[0].rearrange("p t i -> p (t i)").bitcast(I32))
        bias = tile("bias", [P, N_TILES], F32)
        with nc.allow_non_contiguous_dma(reason="one bias value for each partition and tile"):
            nc.sync.dma_start(out=bias[:], in_=bn.rearrange("(c p) -> p c", p=P))


        def load_rows(name, rows):
            raw = tile(name, [P, PACK, rows.shape[1]], F32)
            nc.sync.dma_start(out=raw[:], in_=rows.rearrange("(p j) w -> p j w", j=PACK))
            return raw[:]

        def load_w(c):
            cols = slice(c * P, (c + 1) * P)
            srcs = [un[:, cols], wn[0:K_PASS, cols], wn[K_PASS:K, cols]]
            raw = tile("w%d" % c, [P, 3 * PACK, P], F32)
            parts = [raw[:, a * PACK : (a + 1) * PACK, :] for a in range(3)]
            for part, rows in zip(parts, srcs):
                nc.sync.dma_start(out=part, in_=rows.rearrange("(p j) w -> p j w", j=PACK))
            return parts

        def load_x(a, j0, j1):
            return load_rows("x%d_%d" % (a, j0), x[a * K_PASS : (a + 1) * K_PASS, j0:j1])

        def load_h(c):
            h = tile("h%d" % c, [P, T], F32)
            nc.sync.dma_start(out=h[:], in_=hT[c * P : (c + 1) * P, :])
            return h

        gain = tile("gain", [P, J], F32)
        w_raw, h_in, x_raw = {}, {}, {}

        def load_x_quarter(b):
            x_raw[b] = [load_x(a, b * Q, (b + 1) * Q) for a in range(2)]

        w_raw[0] = load_w(0)
        load_x_quarter(0)
        load_x_quarter(1)
        h_in[0] = load_h(0)
        nc.sync.dma_start(out=gain[:, 0:Q], in_=wgo[:, 0:Q])
        w_raw[1] = load_w(1)
        nc.sync.dma_start(out=gain[:, Q : 2 * Q], in_=wgo[:, Q : 2 * Q])
        h_in[1] = load_h(1)
        load_x_quarter(2)
        nc.sync.dma_start(out=gain[:, 2 * Q : J], in_=wgo[:, 2 * Q : J])
        load_x_quarter(3)
        w_raw[2] = load_w(2)
        w_raw[3] = load_w(3)
        h_in[2] = load_h(2)
        h_in[3] = load_h(3)

        def weave(name, raws, codes, scales, tag):
            width = raws[0].shape[2] * PACK
            woven = tile(name, [P, len(raws) * width], BF16, tag)
            steps = []
            for a, raw in enumerate(raws):
                part = woven[:, a * width : (a + 1) * width]
                nc.scalar.copy(
                    out=part.rearrange("p (c i t) -> p c t i", i=4, t=PACK),
                    in_=raw.rearrange("p t (c i) -> p c t i", i=4),
                )
                steps.append((codes[a], scales[a], part))
            return steps

        def quantise(steps):
            for codes, scales, part in steps:
                nc.vector.quantize_mx(out=codes.bitcast(FP8X4), scales=scales, in_=part)

        x_codes = [tile("x_codes%d" % a, [P, J], U32) for a in range(2)]
        x_scales = [tile("x_scales%d" % a, [P, J], U8) for a in range(2)]
        w_codes, w_scales = {}, {}

        def weave_w(c, tag=None):
            w_codes[c] = [tile("w_codes%d_%d" % (c, a), [P, P], U32) for a in range(3)]
            w_scales[c] = [tile("w_scales%d_%d" % (c, a), [P, P], U8) for a in range(3)]
            return weave("ww%d" % c, w_raw[c], [t[:] for t in w_codes[c]], [t[:] for t in w_scales[c]], tag)

        def weave_x(b, tag=None):
            cols = slice(b * Q, (b + 1) * Q)
            return weave("xw%d" % b, x_raw[b], [t[:, cols] for t in x_codes], [t[:, cols] for t in x_scales], tag)

        def picks(j0, j1):
            return offsets[:, j0 // 16 : j1 // 16]

        v_codes = tile("v_codes", [P, J], U32)
        v_scales = tile("v_scales", [P, J], U8)
        for q in range(4):
            rows = slice(32 * q, 32 * q + 4)
            nc.vector.tensor_copy(out=plane[rows, :].bitcast(I32), in_=landed[rows, :])
        nc.vector.tensor_copy(out=v_scales[:], in_=plane[:].indirect(offsets[:]))
        nc.vector.tensor_copy(out=v_codes[:], in_=table[:].bitcast(U32).indirect(offsets[:]))
        quantise(weave_w(0))
        quantise(weave_x(0, "w0"))
        quantise(weave_x(1, "x1_0"))
        pages = [tile("page0", [P, T], F32), tile("page1", [P, T], F32)]
        nc.vector.memset(pages[0][:], 0.0)
        nc.vector.memset(pages[1][:], 0.0)
        pages = pages + pages

        acts = {}

        def product(c, j0, j1, tag=None):
            acts[c, j0] = tile("act%d_%d" % (c, j0), [P, j1 - j0], F32, tag)
            step = min(j1 - j0, 2 * Q)
            for n0 in range(j0, j1, step):
                cols = slice(n0, n0 + step)
                acc = psum.tile([P, step], F32, name="acc")
                moving = [(v_codes, v_scales), (x_codes[0], x_scales[0]), (x_codes[1], x_scales[1])]
                for a, (codes, scales) in enumerate(moving):
                    nc.tensor.matmul_mx(
                        out=acc[:],
                        lhsT=w_codes[c][a][:].bitcast(FP8X4),
                        lhsT_scale=w_scales[c][a][:],
                        rhs=codes[:, cols].bitcast(FP8X4),
                        rhs_scale=scales[:, cols],
                        start=(a == 0),
                        stop=(a == 2),
                    )
                nc.scalar.activation(
                    out=acts[c, j0][:, n0 - j0 : n0 - j0 + step], in_=acc[:], func=TANH, bias=bias[:, c : c + 1]
                )

        sums = {}

        def add_state(c, j0, j1, tag=None):
            sums[c, j0] = tile("sum%d_%d" % (c, j0), [P, j1 - j0], F32, tag)
            nc.vector.tensor_tensor(sums[c, j0][:], h_in[c][:].indirect(picks(j0, j1)), acts[c, j0][:], ADD)

        def scatter(c, j0, j1):
            nc.vector.tensor_tensor(pages[c][:].indirect(picks(j0, j1)), sums[c, j0][:], gain[:, j0:j1], MULT)

        def place(c, j0, j1, tag=None):
            add_state(c, j0, j1, tag)
            scatter(c, j0, j1)

        def store(c):
            nc.sync.dma_start(out=out[c * P : (c + 1) * P, :], in_=pages[c][:])

        def place_round(steps, raw_tag, c, j0, j1):
            quantise(steps[:-1])
            add_state(c, j0, j1, raw_tag)
            quantise(steps[-1:])

        product(0, 0, Q, "hold_w1")
        product(0, Q, 2 * Q)
        place(0, 0, Q)
        place_round(weave_w(1, "hold_w1"), "w1", 0, Q, 2 * Q)
        product(1, 0, Q, "hold_xc")
        product(1, Q, 2 * Q, "hold_w2")
        scatter(0, Q, 2 * Q)
        place(1, 0, Q, "hold_xd")
        place_round(weave_x(2, "hold_xc"), "x1_512", 1, Q, 2 * Q)
        product(0, 2 * Q, 3 * Q, "hold_w3")
        scatter(1, Q, 2 * Q)
        place_round(weave_x(3, "hold_xd"), "x1_768", 0, 2 * Q, 3 * Q)
        product(0, 3 * Q, J)
        product(1, 2 * Q, J)
        scatter(0, 2 * Q, 3 * Q)
        place_round(weave_w(2, "hold_w2"), "w2", 0, 3 * Q, J)
        product(2, 0, J)
        scatter(0, 3 * Q, J)
        store(0)
        quantise(weave_w(3, "hold_w3"))
        product(3, 0, J)
        add_state(1, 2 * Q, J, "w3")
        add_state(2, 0, J)
        scatter(1, 2 * Q, J)
        store(1)
        add_state(3, 0, J)
        scatter(2, 0, J)
        store(2)
        scatter(3, 0, J)
        rows = slice(3 * P, N)
        nc.sync.dma_start(out=out[rows, 0 : T // 2], in_=pages[3][:, 0 : T // 2])
        nc.scalar.dma_start(out=out[rows, T // 2 : T], in_=pages[3][:, T // 2 : T])
